import numpy as np
import ml_dtypes


def mxq(x, axis, fmt="e4m3"):
    dtype, down = {"e4m3": (ml_dtypes.float8_e4m3fn, 7), "e5m2": (ml_dtypes.float8_e5m2, 14)}[fmt]
    v = np.moveaxis(np.asarray(x, np.float32).astype(ml_dtypes.bfloat16).astype(np.float64), axis, -1)
    blocks = v.reshape(v.shape[:-1] + (-1, 32))
    amax = np.abs(blocks).max(-1, keepdims=True)
    byte = np.maximum(np.where(amax > 0, np.frexp(amax)[1] - 1 + 127, 0) - down, 1)
    scale = np.exp2(byte - 127.0)
    codes = (blocks / scale).astype(np.float32).astype(dtype).astype(np.float64)
    return np.moveaxis((codes * scale).reshape(v.shape), -1, axis)


WIDE = False


def mx_kscale(k):
    if not WIDE:
        return np.ones(k)
    levels = np.array([10, -10, 5, -5, 0])
    if k % 512:
        return np.exp2(np.random.permutation(np.resize(levels, k // 32))).repeat(32)
    a = np.empty((k // 512, 16))
    for p in range(k // 512):
        a[p, :8] = np.random.permutation(np.resize(levels, 8))
        for g in range(8):
            far = levels[np.abs(levels - a[p, g]) >= 10]
            a[p, g + 8] = far[np.random.randint(len(far))]
    return np.exp2(a.ravel()).repeat(32)


def f64(x):
    return np.asarray(x).astype(np.float64)


def striped(idx):
    return np.tile(idx.reshape(-1, 16).T, (8, 1)).astype(np.uint16)


def unstriped(offs):
    return offs[:16].T.reshape(-1).astype(np.int64)


E2M1 = np.array([0.0, 0.5, 1.0, 1.5, 2.0, 3.0, 4.0, 6.0, -0.0, -0.5, -1.0, -1.5, -2.0, -3.0, -4.0, -6.0])


def pack_weight(w, fmt):
    k, n = w.shape
    w = f64(np.asarray(w, np.float32).astype(ml_dtypes.bfloat16)).reshape(k // 32, 32, n)
    amax = np.abs(w).max(1)
    if fmt == "e4m3":
        byte = np.frexp(amax)[1] - 1 + 127 - 7
    else:
        mant, ex = np.frexp(amax / 6.0)
        byte = np.where(mant > 0.5, ex, ex - 1) + 127
    byte = np.clip(np.where(amax > 0, byte, 1), 1, 254)
    scaled = (w * np.exp2(127.0 - byte)[:, None, :]).reshape(k, n).astype(np.float32)
    by_word = np.ascontiguousarray(scaled.reshape(k // 512, 128, 4, n).transpose(0, 1, 3, 2))
    if fmt == "e4m3":
        words = by_word.astype(ml_dtypes.float8_e4m3fn).view(np.uint8)
    else:
        c = by_word.astype(ml_dtypes.float4_e2m1fn).view(np.uint8) & 0xF
        words = (c[..., 0::2] | (c[..., 1::2] << 4)).reshape(k // 512, 128, 2 * n)
    return np.ascontiguousarray(words), np.ascontiguousarray(byte.astype(np.uint8).reshape(k // 512, 16, n))


def unpack_weight(words, scales, fmt):
    g, _, n = scales.shape
    words = np.ascontiguousarray(words).reshape(g, 128, n, -1)
    if fmt == "e4m3":
        vals = words.view(ml_dtypes.float8_e4m3fn).astype(np.float64)
    else:
        nib = np.empty((g, 128, n, 4), np.uint8)
        nib[..., 0::2] = words & 0xF
        nib[..., 1::2] = words >> 4
        vals = E2M1[nib]
    vals = vals * np.repeat(np.exp2(scales.astype(np.float64) - 127.0), 8, axis=1)[..., None]
    return vals.transpose(0, 1, 3, 2).reshape(g * 512, n)


def gelu(v):
    return 0.5 * v * (1.0 + np.tanh(np.sqrt(2.0 / np.pi) * (v + 0.044715 * v**3)))


K, T, S, H, T2, P = 1536, 2048, 512, 1024, 1024, 512

def setup_inputs():
    n = np.random.standard_normal
    s = mx_kscale(K)[:, None]
    u = mx_kscale(H)[:, None]
    d = {}
    d["tab_words"], d["tab_scales"] = pack_weight(n((K, T)) * s, "e4m3")
    d["offs"] = striped(np.random.permutation(T)[:S])
    d["w1"] = (n((K, H)) / s * u.T / K ** 0.5).astype(np.float32)
    d["w4_words"], d["w4_scales"] = pack_weight(1.5 * n((K, H)) / s / K ** 0.5, "e2m1")
    d["page0"] = (n((H, T2)) * u).astype(np.float32)
    d["wgs"] = np.exp(0.3 * n((128, S))).astype(np.float32)
    d["offs2"] = striped(np.random.permutation(T2)[:S])
    d["offs3"] = striped(np.random.permutation(T2)[:P])
    d["cen"] = (n(H) * u[:, 0]).astype(np.float32)
    d["wv"] = (n(H) / u[:, 0] ** 2 / H ** 0.5).astype(np.float32)
    d["slot"] = (0.8 * n(T2)).astype(np.float32)
    return d

def reference(tab_words, tab_scales, offs, w1, w4_words, w4_scales, page0, wgs, offs2, offs3, cen, wv, slot):
    v = unpack_weight(tab_words, tab_scales, "e4m3")[:, unstriped(offs)]
    w4 = unpack_weight(w4_words, w4_scales, "e2m1")
    a = mxq(f64(w1), 0, "e4m3").T @ v
    b = w4.T @ v
    h = a * np.log(1.0 + b ** 2)
    page = f64(page0).copy()
    page[:, unstriped(offs2)] = np.tile(f64(wgs), (H // 128, 1)) * h
    x = (page[:, unstriped(offs3)] - f64(cen)[:, None]) * f64(wv)[:, None]
    e = mxq(page, 0, "e4m3").T @ mxq(x, 0, "e4m3")
    return np.maximum(e, f64(slot)[:, None])

@@ -1,0 +1,341 @@
+from contextlib import ExitStack
+
+import concourse.mybir as mybir
+
+K, T, S, H, T2, NP = 1536, 2048, 512, 1024, 1024, 512
+FLOPS = 2 * K * H * S * 2 + 2 * H * T2 * NP
+
+F32 = mybir.dt.float32
+BF16 = mybir.dt.bfloat16
+I32 = mybir.dt.int32
+U32 = mybir.dt.uint32
+U16 = mybir.dt.uint16
+U8 = mybir.dt.uint8
+FP8X4 = mybir.dt.float8_e4m3fn_x4
+FP4X4 = mybir.dt.float4_e2m1fn_x4
+ALU = mybir.AluOpType
+ACT = mybir.ActivationFunctionType
+
+P = 128
+PACK = 4
+KP = P * PACK
+KA = K // KP
+HB = H // KP
+MT = T2 // P
+
+
+def tile_list_dive_profile_scores_kernel(
+    tc, tab_words, tab_scales, offs, w1, w4_words, w4_scales, page0, wgs, offs2, offs3, cen, wv, slot, out
+):
+    nc = tc.nc
+    with ExitStack() as ctx:
+        keep = ctx.enter_context(tc.tile_pool(name="keep", bufs=1))
+        ring = ctx.enter_context(tc.tile_pool(name="ring", bufs=1))
+        psum = ctx.enter_context(tc.psum_pool(name="psum", bufs=4))
+
+        idx1 = keep.tile([P, S // 16], U16, name="idx1")
+        idx2 = keep.tile([P, S // 16], U16, name="idx2")
+        idx3 = keep.tile([P, NP // 16], U16, name="idx3")
+
+        tab_sc = keep.tile([P, KA, T], U8, name="tab_sc", align_bytes=64)
+        w4_sc_raw = keep.tile([P, KA, H], U8, name="w4_sc_raw", align_bytes=64)
+        tab_sc_words = tab_sc[:].rearrange("p a n -> p (a n)").bitcast(I32)
+        nc.gpsimd.memset(tab_sc_words[:, 0:768], 0)
+        nc.vector.memset(tab_sc_words[:, 768:], 0)
+        nc.vector.memset(w4_sc_raw[:].bitcast(I32), 0)
+        warm = keep.tile([P, 1], F32, name="warm")
+        nc.gpsimd.memset(warm[:], 1.0)
+        warm2 = keep.tile([P, 1], F32, name="warm2")
+        nc.scalar.activation(out=warm2[:], in_=warm[:], func=ACT.Ln, bias=1.0)
+
+
+        nc.sync.dma_start(idx1[:], offs)
+        nc.sync.dma_start(idx2[:], offs2)
+        nc.sync.dma_start(idx3[:], offs3)
+        cen_sb = keep.tile([P, HB, PACK], F32, name="cen_sb")
+        wv_sb = keep.tile([P, HB, PACK], F32, name="wv_sb")
+        slot_sb = keep.tile([P, MT], F32, name="slot_sb")
+        tab_w = [ring.tile([P, T], U32, name="tab_w%d" % a, tag="t%d" % a, align_bytes=64) for a in range(KA)]
+        w4_raw = [keep.tile([P, KA, H], U8, name="w4_raw%d" % b, align_bytes=64) for b in range(HB)]
+
+        def load_tab(a, lo, hi):
+            nc.sync.dma_start(out=tab_w[a][:, lo:hi].bitcast(I32), in_=tab_words[a].rearrange("p n i -> p (n i)").bitcast(I32)[:, lo:hi])
+
+        def load_w4(b):
+            nc.sync.dma_start(out=w4_raw[b][:].bitcast(I32), in_=w4_words[:, :, b * H : (b + 1) * H].rearrange("a p n -> p a n").bitcast(I32))
+
+        for c in range(4):
+            load_tab(0, c * T // 4, (c + 1) * T // 4)
+        for q in range(4):
+            nc.sync.dma_start(
+                out=tab_sc[32 * q : 32 * q + 4, :, :].bitcast(I32),
+                in_=tab_scales[:, 4 * q : 4 * q + 4, :].rearrange("a r n -> r a n").bitcast(I32),
+            )
+        load_tab(1, 0, T)
+        for q in range(4):
+            nc.sync.dma_start(
+                out=w4_sc_raw[32 * q : 32 * q + 4, :, :].bitcast(I32),
+                in_=w4_scales[:, 4 * q : 4 * q + 4, :].rearrange("a r n -> r a n").bitcast(I32),
+            )
+        load_tab(2, 0, T)
+        wg = keep.tile([P, PACK, S], F32, name="wg")
+
+        w1_raw = {}
+
+        def load_w1(a, b):
+            raw = ring.tile([P, PACK, KP], F32, name="w1_raw%d%d" % (a, b), tag=("w%d" if b == 0 else "t%d") % a, align_bytes=64)
+            nc.sync.dma_start(
+                out=raw[:], in_=w1[a * KP : (a + 1) * KP, b * KP : (b + 1) * KP].rearrange("(p j) c -> p j c", j=PACK)
+            )
+            w1_raw[(a, b)] = raw
+
+        page = {}
+
+        def load_page(s):
+            b, t = divmod(s, PACK)
+            pg = keep.tile([P, T2], F32, name="page%d" % s)
+            nc.sync.dma_start(out=pg[:], in_=page0[b * KP : (b + 1) * KP, :].rearrange("(p t) m -> p t m", t=PACK)[:, t, :])
+            page[s] = pg
+
+        load_w1(0, 0)
+        load_w1(1, 0)
+        load_w4(0)
+        load_w1(2, 0)
+        load_w4(1)
+        for q in range(4):
+            nc.sync.dma_start(out=wg[32 * q : 32 * q + 32, :, :], in_=wgs.rearrange("(p t) j -> p t j", t=PACK))
+        load_page(0)
+        load_page(1)
+        load_w1(0, 1)
+        load_w1(1, 1)
+        load_page(2)
+        load_w1(2, 1)
+        nc.sync.dma_start(out=cen_sb[:], in_=cen.rearrange("(b p t) -> p b t", b=HB, t=PACK))
+        nc.sync.dma_start(out=wv_sb[:], in_=wv.rearrange("(b p t) -> p b t", b=HB, t=PACK))
+        for s in range(3, HB * PACK):
+            load_page(s)
+        with nc.allow_non_contiguous_dma(reason="one bound for each partition"):
+            nc.sync.dma_start(out=slot_sb[:], in_=slot.rearrange("(c p) -> p c", p=P))
+
+        v_w = keep.tile([P, KA, S], U32, name="v_w", align_bytes=64)
+        v_sc = keep.tile([P, KA, S], U8, name="v_sc", align_bytes=64)
+        w4_w = keep.tile([P, KA, 2 * H], U8, name="w4_w", align_bytes=64)
+        w4_sc = keep.tile([P, KA, H], U8, name="w4_sc", align_bytes=64)
+
+        def deal_words(b):
+            nc.vector.tensor_copy(
+                out=w4_w[:].bitcast(U16).rearrange("p a (b t m) -> p b a t m", b=HB, t=PACK)[:, b],
+                in_=w4_raw[b][:].bitcast(U16).rearrange("p a (m t) -> p a t m", t=PACK),
+            )
+
+        def deal_scales(b):
+            nc.vector.tensor_copy(
+                out=w4_sc[:].rearrange("p a (b t m) -> p b a t m", b=HB, t=PACK)[:, b],
+                in_=w4_sc_raw[:].rearrange("p a (b m t) -> p b a t m", b=HB, t=PACK)[:, b],
+            )
+
+        def gather_words(a):
+            nc.vector.tensor_copy(v_w[:, a, :], tab_w[a][:].indirect(idx1[:]))
+
+        def gather_scales(a):
+            nc.vector.tensor_copy(v_sc[:, a, :], tab_sc[:, a, :].indirect(idx1[:]))
+
+        gather_words(0)
+        gather_scales(0)
+        gather_scales(1)
+        gather_words(1)
+        gather_scales(2)
+        deal_scales(0)
+        gather_words(2)
+        deal_scales(1)
+
+        w1_w = keep.tile([P, KA, HB, KP], U32, name="w1_w", align_bytes=64)
+        w1_sc = keep.tile([P, KA, HB, KP], U8, name="w1_sc", align_bytes=64)
+
+        def quantise_w1(a, b, wbf):
+            nc.vector.quantize_mx(out=w1_w[:, a, b, :].bitcast(FP8X4), scales=w1_sc[:, a, b, :], in_=wbf[:])
+
+        def prep_w1(a, b):
+            wbf = ring.tile([P, KP * PACK], BF16, name="wbf", tag="bf", bufs=3, align_bytes=64)
+            dst = wbf[:].rearrange("p (t m j) -> p m j t", t=PACK, j=PACK)
+            src = w1_raw[(a, b)][:].rearrange("p j (m t) -> p m j t", t=PACK)
+            if b == 0 and a == KA - 1:
+                nc.vector.tensor_copy(out=dst[:, :, :, 0], in_=src[:, :, :, 0])
+                nc.vector.quantize_mx(out=w1_w[:, a, b, 0:P].bitcast(FP8X4), scales=w1_sc[:, a, b, 0:P], in_=wbf[:, 0:KP])
+                nc.vector.tensor_copy(out=dst[:, :, :, 1:PACK], in_=src[:, :, :, 1:PACK])
+                nc.vector.quantize_mx(out=w1_w[:, a, b, P : 2 * P].bitcast(FP8X4), scales=w1_sc[:, a, b, P : 2 * P], in_=wbf[:, KP : 2 * KP])
+                nc.vector.quantize_mx(out=w1_w[:, a, b, 2 * P :].bitcast(FP8X4), scales=w1_sc[:, a, b, 2 * P :], in_=wbf[:, 2 * KP :])
+                return
+            nc.scalar.copy(out=dst, in_=src)
+            quantise_w1(a, b, wbf)
+
+        a_sb = {}
+
+        def first_product(s):
+            b, t = divmod(s, PACK)
+            acc = psum.tile([P, S], F32, name="acc", tag="pa")
+            for a in range(KA):
+                nc.tensor.matmul_mx(
+                    out=acc[:], lhsT=w1_w[:, a, b, t * P : (t + 1) * P].bitcast(FP8X4), lhsT_scale=w1_sc[:, a, b, t * P : (t + 1) * P],
+                    rhs=v_w[:, a, :].bitcast(FP8X4), rhs_scale=v_sc[:, a, :], start=(a == 0), stop=(a == KA - 1),
+                )
+            sb = ring.tile([P, S], F32, name="a_sb", tag="a_sb", bufs=4, align_bytes=64)
+            nc.scalar.copy(out=sb[:], in_=acc[:])
+            a_sb[s] = sb
+
+        lw = {}
+
+        def second_product(s):
+            b, t = divmod(s, PACK)
+            acc = psum.tile([P, S], F32, name="acc", tag="pb")
+            for a in range(KA):
+                nc.tensor.matmul_mx(
+                    out=acc[:], lhsT=w4_w[:, a, s * 2 * P : (s + 1) * 2 * P].bitcast(FP4X4), lhsT_scale=w4_sc[:, a, s * P : (s + 1) * P],
+                    rhs=v_w[:, a, :].bitcast(FP8X4), rhs_scale=v_sc[:, a, :], start=(a == 0), stop=(a == KA - 1),
+                )
+            sq = ring.tile([P, S], F32, name="sq", tag="sq", bufs=2)
+            nc.scalar.activation(out=sq[:], in_=acc[:], func=ACT.Square)
+            f = ring.tile([P, S], F32, name="lw", tag="h%d" % s, align_bytes=64)
+            nc.scalar.activation(out=f[:], in_=sq[:], func=ACT.Ln, bias=1.0)
+            lw[s] = f
+
+        def weigh(s):
+            nc.vector.tensor_tensor(out=lw[s][:], in0=lw[s][:], in1=wg[:, s % PACK, :], op=ALU.mult)
+
+        prep_w1(0, 0)
+        prep_w1(1, 0)
+        deal_words(0)
+        second_product(0)
+        prep_w1(2, 0)
+        second_product(1)
+        weigh(0)
+        deal_words(1)
+        weigh(1)
+        first_product(0)
+        first_product(1)
+
+        nb = keep.tile([P, HB, PACK], F32, name="nb")
+
+        p_w = keep.tile([P, HB, T2], U32, name="p_w", align_bytes=64)
+        x_w = keep.tile([P, HB, NP], U32, name="x_w", align_bytes=64)
+        p_sc = {1: keep.tile([P, T2], U8, name="p_sc1", align_bytes=64)}
+        x_sc = {1: keep.tile([P, NP], U8, name="x_sc1", align_bytes=64)}
+        CH = 256
+
+        def put(s):
+            nc.vector.tensor_tensor(page[s][:].indirect(idx2[:]), a_sb[s][:], lw[s][:], ALU.mult)
+
+        def fetch(s, xg):
+            nc.vector.tensor_copy(xg[:, s % PACK, :], page[s][:].indirect(idx3[:]))
+
+        def centre(s, xc, xg):
+            b, t = divmod(s, PACK)
+            nc.scalar.activation(out=xc[:, t, :], in_=xg[:, t, :], func=ACT.Identity, bias=nb[:, b, t : t + 1], scale=wv_sb[:, b, t : t + 1])
+
+        def weave(copy, dst, src):
+            copy(out=dst.rearrange("p (c i t) -> p c t i", i=4, t=PACK), in_=src.rearrange("p t (c i) -> p c t i", i=4))
+
+        def quantise_page(b, pbf, c):
+            nc.vector.quantize_mx(
+                out=p_w[:, b, c * CH : (c + 1) * CH].bitcast(FP8X4), scales=p_sc[b][:, c * CH : (c + 1) * CH],
+                in_=pbf[:, c * CH * PACK : (c + 1) * CH * PACK],
+            )
+
+        stage0 = ring.tile([P, PACK, T2], F32, name="stage", tag="stage", bufs=2)
+        stage1 = ring.tile([P, PACK, T2], F32, name="stage", tag="stage", bufs=2)
+        xg0 = ring.tile([P, PACK, NP], F32, name="xg", tag="w0", align_bytes=64)
+        xg1 = ring.tile([P, PACK, NP], F32, name="xg", tag="w1", align_bytes=64)
+
+        def step(s, xg, stage):
+            put(s)
+            nc.gpsimd.dma_start(out=stage[:, s % PACK, :], in_=page[s][:])
+            fetch(s, xg)
+
+        step(0, xg0, stage0)
+        step(1, xg0, stage0)
+        second_product(2)
+        weigh(2)
+        first_product(2)
+        step(2, xg0, stage0)
+        prep_w1(0, 1)
+        prep_w1(1, 1)
+        second_product(3)
+        weigh(3)
+        prep_w1(2, 1)
+        first_product(3)
+        step(3, xg0, stage0)
+        nc.vector.scalar_tensor_tensor(out=nb[:], in0=cen_sb[:], scalar=-1.0, in1=wv_sb[:], op0=ALU.mult, op1=ALU.mult)
+        second_product(4)
+        weigh(4)
+        first_product(4)
+        xc = ring.tile([P, PACK, NP], BF16, name="xc", tag="t2", align_bytes=64)
+        for s in range(PACK - 1):
+            centre(s, xc, xg0)
+        step(4, xg1, stage1)
+        second_product(5)
+        weigh(5)
+        first_product(5)
+        centre(3, xc, xg0)
+        second_product(6)
+        weigh(6)
+        first_product(6)
+        xbf0 = ring.tile([P, NP * PACK], BF16, name="xbf", tag="bf", bufs=3, align_bytes=64)
+        weave(nc.scalar.copy, xbf0[:], xc[:])
+        second_product(7)
+        weigh(7)
+        first_product(7)
+        pbf0 = ring.tile([P, T2 * PACK], BF16, name="pbf", tag="pbf", align_bytes=64)
+        for c in range(T2 // CH):
+            weave(nc.scalar.copy, pbf0[:, c * CH * PACK : (c + 1) * CH * PACK], stage0[:, :, c * CH : (c + 1) * CH])
+        step(5, xg1, stage1)
+        centre(4, xc, xg1)
+        centre(5, xc, xg1)
+        x_sc[0] = ring.tile([P, NP], U8, name="x_sc0", tag="h5", align_bytes=64)
+        p_sc[0] = ring.tile([P, T2], U8, name="p_sc0", tag="h6", align_bytes=64)
+        nc.vector.quantize_mx(out=x_w[:, 0, :].bitcast(FP8X4), scales=x_sc[0][:], in_=xbf0[:])
+        put(6)
+        nc.scalar.copy(out=stage1[:, 2, :], in_=page[6][:])
+        fetch(6, xg1)
+        nc.vector.quantize_mx(out=p_w[:, 0, :].bitcast(FP8X4), scales=p_sc[0][:], in_=pbf0[:])
+        centre(6, xc, xg1)
+        xbf1 = ring.tile([P, NP * PACK], BF16, name="xbf", tag="bf", bufs=3, align_bytes=64)
+        weave(nc.scalar.copy, xbf1[:], xc[:])
+        put(7)
+        fetch(7, xg1)
+        nc.vector.tensor_scalar(
+            out=xbf1[:].rearrange("p (c t) -> p c t", t=PACK)[:, :, 3], in0=xg1[:, 3, :],
+            scalar1=cen_sb[:, 1, 3:4], scalar2=wv_sb[:, 1, 3:4], op0=ALU.subtract, op1=ALU.mult,
+        )
+        nc.vector.quantize_mx(out=x_w[:, 1, :].bitcast(FP8X4), scales=x_sc[1][:], in_=xbf1[:])
+        pbf1 = ring.tile([P, T2 * PACK], BF16, name="pbf", tag="pbf", align_bytes=64)
+
+        def finish_page(copy, c):
+            copy(out=stage1[:, 3, c * CH : (c + 1) * CH], in_=page[7][:, c * CH : (c + 1) * CH])
+            weave(copy, pbf1[:, c * CH * PACK : (c + 1) * CH * PACK], stage1[:, :, c * CH : (c + 1) * CH])
+
+        finish_page(nc.scalar.copy, 0)
+        quantise_page(1, pbf1, 0)
+        finish_page(nc.scalar.copy, 1)
+        finish_page(nc.vector.tensor_copy, 3)
+        quantise_page(1, pbf1, 1)
+        quantise_page(1, pbf1, 3)
+        finish_page(nc.scalar.copy, 2)
+        quantise_page(1, pbf1, 2)
+
+        for mt in (0, 1, 2, 3, 6, 7, 4, 5):
+            acc = psum.tile([P, NP], F32, name="acc", tag="pb" if mt < MT // 2 else "pa")
+            for b in range(HB):
+                nc.tensor.matmul_mx(
+                    out=acc[:], lhsT=p_w[:, b, mt * P : (mt + 1) * P].bitcast(FP8X4), lhsT_scale=p_sc[b][:, mt * P : (mt + 1) * P],
+                    rhs=x_w[:, b, :].bitcast(FP8X4), rhs_scale=x_sc[b][:], start=(b == 0), stop=(b == HB - 1),
+                )
+            if mt < MT // 2:
+                res = ring.tile([P, NP], F32, name="res", tag="h%d" % mt, align_bytes=64)
+            else:
+                res = ring.tile([P, NP], F32, name="res", tag="a_sb", bufs=4, align_bytes=64)
+            if mt % 2 == 0:
+                nc.scalar.copy(out=res[:], in_=acc[:])
+                nc.vector.tensor_scalar(out=res[:], in0=res[:], scalar1=slot_sb[:, mt : mt + 1], scalar2=None, op0=ALU.max)
+            else:
+                nc.vector.tensor_scalar(out=res[:], in0=acc[:], scalar1=slot_sb[:, mt : mt + 1], scalar2=None, op0=ALU.max)
+            nc.sync.dma_start(out=out[mt * P : (mt + 1) * P, :], in_=res[:])

@@ -56,13 +56,10 @@ def tile_list_dive_profile_scores_kernel(
         wv_sb = keep.tile([P, HB, PACK], F32, name="wv_sb")
         slot_sb = keep.tile([P, MT], F32, name="slot_sb")
         tab_w = [ring.tile([P, T], U32, name="tab_w%d" % a, tag="t%d" % a, align_bytes=64) for a in range(KA)]
-        w4_raw = [keep.tile([P, KA, H], U8, name="w4_raw%d" % b, align_bytes=64) for b in range(HB)]
+        w4_raw = keep.tile([P, KA, 2 * H], U8, name="w4_raw", align_bytes=64)
 
         def load_tab(a, lo, hi):
             nc.sync.dma_start(out=tab_w[a][:, lo:hi].bitcast(I32), in_=tab_words[a].rearrange("p n i -> p (n i)").bitcast(I32)[:, lo:hi])
-
-        def load_w4(b):
-            nc.sync.dma_start(out=w4_raw[b][:].bitcast(I32), in_=w4_words[:, :, b * H : (b + 1) * H].rearrange("a p n -> p a n").bitcast(I32))
 
         for c in range(4):
             load_tab(0, c * T // 4, (c + 1) * T // 4)
@@ -78,7 +75,11 @@ def tile_list_dive_profile_scores_kernel(
                 in_=w4_scales[:, 4 * q : 4 * q + 4, :].rearrange("a r n -> r a n").bitcast(I32),
             )
         load_tab(2, 0, T)
-        wg = keep.tile([P, PACK, S], F32, name="wg")
+        wg = [keep.tile([P, 2, S], F32, name="wg%d" % u) for u in range(2)]
+
+        def load_wg(u):
+            for q in range(4):
+                nc.sync.dma_start(out=wg[u][32 * q : 32 * q + 32, :, :], in_=wgs.rearrange("(p t) j -> p t j", t=PACK)[:, 2 * u : 2 * u + 2, :])
 
         w1_raw = {}
 
@@ -99,13 +100,12 @@ def tile_list_dive_profile_scores_kernel(
 
         load_w1(0, 0)
         load_w1(1, 0)
-        load_w4(0)
+        nc.sync.dma_start(out=w4_raw[:].bitcast(I32), in_=w4_words.rearrange("a p n -> p a n").bitcast(I32))
         load_w1(2, 0)
-        load_w4(1)
-        for q in range(4):
-            nc.sync.dma_start(out=wg[32 * q : 32 * q + 32, :, :], in_=wgs.rearrange("(p t) j -> p t j", t=PACK))
+        load_wg(0)
         load_page(0)
         load_page(1)
+        load_wg(1)
         load_w1(0, 1)
         load_w1(1, 1)
         load_page(2)
@@ -125,7 +125,7 @@ def tile_list_dive_profile_scores_kernel(
         def deal_words(b):
             nc.vector.tensor_copy(
                 out=w4_w[:].bitcast(U16).rearrange("p a (b t m) -> p b a t m", b=HB, t=PACK)[:, b],
-                in_=w4_raw[b][:].bitcast(U16).rearrange("p a (m t) -> p a t m", t=PACK),
+                in_=w4_raw[:].bitcast(U16).rearrange("p a (b m t) -> p b a t m", b=HB, t=PACK)[:, b],
             )
 
         def deal_scales(b):
@@ -162,16 +162,19 @@ def tile_list_dive_profile_scores_kernel(
             if b == 0 and a == KA - 1:
                 nc.vector.tensor_copy(out=dst[:, :, :, 0], in_=src[:, :, :, 0])
                 nc.vector.quantize_mx(out=w1_w[:, a, b, 0:P].bitcast(FP8X4), scales=w1_sc[:, a, b, 0:P], in_=wbf[:, 0:KP])
-                nc.vector.tensor_copy(out=dst[:, :, :, 1:PACK], in_=src[:, :, :, 1:PACK])
-                nc.vector.quantize_mx(out=w1_w[:, a, b, P : 2 * P].bitcast(FP8X4), scales=w1_sc[:, a, b, P : 2 * P], in_=wbf[:, KP : 2 * KP])
-                nc.vector.quantize_mx(out=w1_w[:, a, b, 2 * P :].bitcast(FP8X4), scales=w1_sc[:, a, b, 2 * P :], in_=wbf[:, 2 * KP :])
-                return
+
+                def rest():
+                    nc.vector.tensor_copy(out=dst[:, :, :, 1:PACK], in_=src[:, :, :, 1:PACK])
+                    nc.vector.quantize_mx(out=w1_w[:, a, b, P : 2 * P].bitcast(FP8X4), scales=w1_sc[:, a, b, P : 2 * P], in_=wbf[:, KP : 2 * KP])
+                    nc.vector.quantize_mx(out=w1_w[:, a, b, 2 * P :].bitcast(FP8X4), scales=w1_sc[:, a, b, 2 * P :], in_=wbf[:, 2 * KP :])
+
+                return rest
             nc.scalar.copy(out=dst, in_=src)
             quantise_w1(a, b, wbf)
 
-        a_sb = {}
+        h = {}
 
-        def first_product(s):
+        def first_product(s, after=None):
             b, t = divmod(s, PACK)
             acc = psum.tile([P, S], F32, name="acc", tag="pa")
             for a in range(KA):
@@ -179,9 +182,8 @@ def tile_list_dive_profile_scores_kernel(
                     out=acc[:], lhsT=w1_w[:, a, b, t * P : (t + 1) * P].bitcast(FP8X4), lhsT_scale=w1_sc[:, a, b, t * P : (t + 1) * P],
                     rhs=v_w[:, a, :].bitcast(FP8X4), rhs_scale=v_sc[:, a, :], start=(a == 0), stop=(a == KA - 1),
                 )
-            sb = ring.tile([P, S], F32, name="a_sb", tag="a_sb", bufs=4, align_bytes=64)
-            nc.scalar.copy(out=sb[:], in_=acc[:])
-            a_sb[s] = sb
+            h[s] = lw[s] if after is None else ring.tile([P, S], F32, name="h", tag=after, align_bytes=64)
+            nc.vector.tensor_tensor(out=h[s][:], in0=acc[:], in1=lw[s][:], op=ALU.mult)
 
         lw = {}
 
@@ -199,31 +201,23 @@ def tile_list_dive_profile_scores_kernel(
             nc.scalar.activation(out=f[:], in_=sq[:], func=ACT.Ln, bias=1.0)
             lw[s] = f
 
-        def weigh(s):
-            nc.vector.tensor_tensor(out=lw[s][:], in0=lw[s][:], in1=wg[:, s % PACK, :], op=ALU.mult)
-
         prep_w1(0, 0)
         prep_w1(1, 0)
         deal_words(0)
         second_product(0)
-        prep_w1(2, 0)
-        second_product(1)
-        weigh(0)
-        deal_words(1)
-        weigh(1)
+        rest_of_w1 = prep_w1(2, 0)
         first_product(0)
-        first_product(1)
+        second_product(1)
 
-        nb = keep.tile([P, HB, PACK], F32, name="nb")
 
         p_w = keep.tile([P, HB, T2], U32, name="p_w", align_bytes=64)
         x_w = keep.tile([P, HB, NP], U32, name="x_w", align_bytes=64)
-        p_sc = {1: keep.tile([P, T2], U8, name="p_sc1", align_bytes=64)}
-        x_sc = {1: keep.tile([P, NP], U8, name="x_sc1", align_bytes=64)}
+        p_sc = [keep.tile([P, T2], U8, name="p_sc%d" % b, align_bytes=64) for b in range(HB)]
+        x_sc = [keep.tile([P, NP], U8, name="x_sc%d" % b, align_bytes=64) for b in range(HB)]
         CH = 256
 
         def put(s):
-            nc.vector.tensor_tensor(page[s][:].indirect(idx2[:]), a_sb[s][:], lw[s][:], ALU.mult)
+            nc.vector.tensor_tensor(page[s][:].indirect(idx2[:]), h[s][:], wg[s % PACK // 2][:, s % 2, :], ALU.mult)
 
         def fetch(s, xg):
             nc.vector.tensor_copy(xg[:, s % PACK, :], page[s][:].indirect(idx3[:]))
@@ -241,99 +235,95 @@ def tile_list_dive_profile_scores_kernel(
                 in_=pbf[:, c * CH * PACK : (c + 1) * CH * PACK],
             )
 
-        stage0 = ring.tile([P, PACK, T2], F32, name="stage", tag="stage", bufs=2)
-        stage1 = ring.tile([P, PACK, T2], F32, name="stage", tag="stage", bufs=2)
+        stage0 = ring.tile([P, PACK, T2], F32, name="stage0", tag="stage0", align_bytes=64)
+        stage1 = [ring.tile([P, 2, T2], F32, name="stage1%d" % u) for u in range(2)]
         xg0 = ring.tile([P, PACK, NP], F32, name="xg", tag="w0", align_bytes=64)
         xg1 = ring.tile([P, PACK, NP], F32, name="xg", tag="w1", align_bytes=64)
 
-        def step(s, xg, stage):
+        def step(s, xg, staged):
             put(s)
-            nc.gpsimd.dma_start(out=stage[:, s % PACK, :], in_=page[s][:])
+            nc.sync.dma_start(out=staged, in_=page[s][:])
             fetch(s, xg)
 
-        step(0, xg0, stage0)
-        step(1, xg0, stage0)
+        def weave_pair(u, lo, hi):
+            nc.scalar.copy(
+                out=pbf1[:, lo * PACK : hi * PACK].rearrange("p (c i u e) -> p u c e i", i=4, u=2, e=2)[:, u],
+                in_=stage1[u][:, :, lo:hi].rearrange("p e (c i) -> p c e i", i=4),
+            )
+
+        step(0, xg0, stage0[:, 0, :])
+        rest_of_w1()
+        deal_words(1)
+        first_product(1)
+        step(1, xg0, stage0[:, 1, :])
         second_product(2)
-        weigh(2)
         first_product(2)
-        step(2, xg0, stage0)
-        prep_w1(0, 1)
-        prep_w1(1, 1)
+        step(2, xg0, stage0[:, 2, :])
+        for a in range(KA):
+            prep_w1(a, 1)
         second_product(3)
-        weigh(3)
-        prep_w1(2, 1)
         first_product(3)
-        step(3, xg0, stage0)
+        step(3, xg0, stage0[:, 3, :])
+        nb = ring.tile([P, HB, PACK], F32, name="nb", tag="h2", align_bytes=64)
         nc.vector.scalar_tensor_tensor(out=nb[:], in0=cen_sb[:], scalar=-1.0, in1=wv_sb[:], op0=ALU.mult, op1=ALU.mult)
         second_product(4)
-        weigh(4)
         first_product(4)
-        xc = ring.tile([P, PACK, NP], BF16, name="xc", tag="t2", align_bytes=64)
-        for s in range(PACK - 1):
-            centre(s, xc, xg0)
-        step(4, xg1, stage1)
         second_product(5)
-        weigh(5)
+        xc0 = ring.tile([P, PACK, NP], BF16, name="xc0", tag="t2", align_bytes=64)
+        for s in range(PACK - 1):
+            centre(s, xc0, xg0)
+        step(4, xg1, stage1[0][:, 0, :])
         first_product(5)
-        centre(3, xc, xg0)
         second_product(6)
-        weigh(6)
-        first_product(6)
-        xbf0 = ring.tile([P, NP * PACK], BF16, name="xbf", tag="bf", bufs=3, align_bytes=64)
-        weave(nc.scalar.copy, xbf0[:], xc[:])
+        centre(3, xc0, xg0)
+        xbf0 = ring.tile([P, NP * PACK], BF16, name="xbf0", tag="xbf0", align_bytes=64)
+        weave(nc.scalar.copy, xbf0[:], xc0[:])
         second_product(7)
-        weigh(7)
-        first_product(7)
-        pbf0 = ring.tile([P, T2 * PACK], BF16, name="pbf", tag="pbf", align_bytes=64)
+        pbf0 = ring.tile([P, T2 * PACK], BF16, name="pbf0", tag="pbf0", align_bytes=64)
         for c in range(T2 // CH):
             weave(nc.scalar.copy, pbf0[:, c * CH * PACK : (c + 1) * CH * PACK], stage0[:, :, c * CH : (c + 1) * CH])
-        step(5, xg1, stage1)
-        centre(4, xc, xg1)
-        centre(5, xc, xg1)
-        x_sc[0] = ring.tile([P, NP], U8, name="x_sc0", tag="h5", align_bytes=64)
-        p_sc[0] = ring.tile([P, T2], U8, name="p_sc0", tag="h6", align_bytes=64)
+        step(5, xg1, stage1[0][:, 1, :])
         nc.vector.quantize_mx(out=x_w[:, 0, :].bitcast(FP8X4), scales=x_sc[0][:], in_=xbf0[:])
-        put(6)
-        nc.scalar.copy(out=stage1[:, 2, :], in_=page[6][:])
-        fetch(6, xg1)
+        first_product(6, after="xbf0")
+        x_late = ring.tile([P, (2 + PACK) * NP], BF16, name="x_late", tag="stage0", align_bytes=64)
+        xc1 = x_late[:, 0 : 2 * NP].rearrange("p (e c) -> p e c", e=2)
+        xbf1 = x_late[:, 2 * NP :]
+        centre(4, xc1, xg1)
+        centre(5, xc1, xg1)
+        pbf1 = ring.tile([P, T2 * PACK], BF16, name="pbf1", align_bytes=64)
+        weave_pair(0, 0, T2)
+        step(6, xg1, stage1[1][:, 0, :])
         nc.vector.quantize_mx(out=p_w[:, 0, :].bitcast(FP8X4), scales=p_sc[0][:], in_=pbf0[:])
-        centre(6, xc, xg1)
-        xbf1 = ring.tile([P, NP * PACK], BF16, name="xbf", tag="bf", bufs=3, align_bytes=64)
-        weave(nc.scalar.copy, xbf1[:], xc[:])
+        first_product(7, after="pbf0")
+        nc.scalar.copy(
+            out=xbf1.rearrange("p (c i u e) -> p u c e i", i=4, u=2, e=2)[:, 0],
+            in_=xc1.rearrange("p e (c i) -> p c e i", i=4),
+        )
+        nc.scalar.activation(
+            out=xbf1.rearrange("p (c t) -> p c t", t=PACK)[:, :, 2:4], in_=xg1[:, 2, :].unsqueeze(2).to_broadcast([P, NP, 2]),
+            func=ACT.Identity, bias=nb[:, 1, 2:3], scale=wv_sb[:, 1, 2:3],
+        )
         put(7)
         fetch(7, xg1)
         nc.vector.tensor_scalar(
-            out=xbf1[:].rearrange("p (c t) -> p c t", t=PACK)[:, :, 3], in0=xg1[:, 3, :],
+            out=xbf1.rearrange("p (c t) -> p c t", t=PACK)[:, :, 3], in0=xg1[:, 3, :],
             scalar1=cen_sb[:, 1, 3:4], scalar2=wv_sb[:, 1, 3:4], op0=ALU.subtract, op1=ALU.mult,
         )
-        nc.vector.quantize_mx(out=x_w[:, 1, :].bitcast(FP8X4), scales=x_sc[1][:], in_=xbf1[:])
-        pbf1 = ring.tile([P, T2 * PACK], BF16, name="pbf", tag="pbf", align_bytes=64)
+        nc.vector.quantize_mx(out=x_w[:, 1, :].bitcast(FP8X4), scales=x_sc[1][:], in_=xbf1)
+        for c in range(T2 // CH):
+            nc.scalar.copy(out=stage1[1][:, 1, c * CH : (c + 1) * CH], in_=page[7][:, c * CH : (c + 1) * CH])
+            weave_pair(1, c * CH, (c + 1) * CH)
+            quantise_page(1, pbf1, c)
 
-        def finish_page(copy, c):
-            copy(out=stage1[:, 3, c * CH : (c + 1) * CH], in_=page[7][:, c * CH : (c + 1) * CH])
-            weave(copy, pbf1[:, c * CH * PACK : (c + 1) * CH * PACK], stage1[:, :, c * CH : (c + 1) * CH])
-
-        finish_page(nc.scalar.copy, 0)
-        quantise_page(1, pbf1, 0)
-        finish_page(nc.scalar.copy, 1)
-        finish_page(nc.vector.tensor_copy, 3)
-        quantise_page(1, pbf1, 1)
-        quantise_page(1, pbf1, 3)
-        finish_page(nc.scalar.copy, 2)
-        quantise_page(1, pbf1, 2)
-
-        for mt in (0, 1, 2, 3, 6, 7, 4, 5):
+        for mt in range(MT):
             acc = psum.tile([P, NP], F32, name="acc", tag="pb" if mt < MT // 2 else "pa")
             for b in range(HB):
                 nc.tensor.matmul_mx(
                     out=acc[:], lhsT=p_w[:, b, mt * P : (mt + 1) * P].bitcast(FP8X4), lhsT_scale=p_sc[b][:, mt * P : (mt + 1) * P],
                     rhs=x_w[:, b, :].bitcast(FP8X4), rhs_scale=x_sc[b][:], start=(b == 0), stop=(b == HB - 1),
                 )
-            if mt < MT // 2:
-                res = ring.tile([P, NP], F32, name="res", tag="h%d" % mt, align_bytes=64)
-            else:
-                res = ring.tile([P, NP], F32, name="res", tag="a_sb", bufs=4, align_bytes=64)
-            if mt % 2 == 0:
+            res = ring.tile([P, NP], F32, name="res", tag="h%d" % mt, align_bytes=64)
+            if mt >= 3:
                 nc.scalar.copy(out=res[:], in_=acc[:])
                 nc.vector.tensor_scalar(out=res[:], in0=res[:], scalar1=slot_sb[:, mt : mt + 1], scalar2=None, op0=ALU.max)
             else:

@@ -31,7 +31,7 @@ def tile_list_dive_profile_scores_kernel(
     with ExitStack() as ctx:
         keep = ctx.enter_context(tc.tile_pool(name="keep", bufs=1))
         ring = ctx.enter_context(tc.tile_pool(name="ring", bufs=1))
-        psum = ctx.enter_context(tc.psum_pool(name="psum", bufs=4))
+        psum = ctx.enter_context(tc.psum_pool(name="psum", bufs=2))
 
         idx1 = keep.tile([P, S // 16], U16, name="idx1")
         idx2 = keep.tile([P, S // 16], U16, name="idx2")
@@ -63,23 +63,24 @@ def tile_list_dive_profile_scores_kernel(
 
         for c in range(4):
             load_tab(0, c * T // 4, (c + 1) * T // 4)
-        for q in range(4):
+        for r in range(4):
             nc.sync.dma_start(
-                out=tab_sc[32 * q : 32 * q + 4, :, :].bitcast(I32),
-                in_=tab_scales[:, 4 * q : 4 * q + 4, :].rearrange("a r n -> r a n").bitcast(I32),
+                out=tab_sc[r:P:32, :, :].bitcast(I32), in_=tab_scales.rearrange("a (q r) n -> r q a n", r=4)[r].bitcast(I32)
             )
         load_tab(1, 0, T)
-        for q in range(4):
+        for r in range(4):
             nc.sync.dma_start(
-                out=w4_sc_raw[32 * q : 32 * q + 4, :, :].bitcast(I32),
-                in_=w4_scales[:, 4 * q : 4 * q + 4, :].rearrange("a r n -> r a n").bitcast(I32),
+                out=w4_sc_raw[r:P:32, :, :].bitcast(I32), in_=w4_scales.rearrange("a (q r) n -> r q a n", r=4)[r].bitcast(I32)
             )
         load_tab(2, 0, T)
-        wg = [keep.tile([P, 2, S], F32, name="wg%d" % u) for u in range(2)]
+        wg = {}
 
-        def load_wg(u):
-            for q in range(4):
-                nc.sync.dma_start(out=wg[u][32 * q : 32 * q + 32, :, :], in_=wgs.rearrange("(p t) j -> p t j", t=PACK)[:, 2 * u : 2 * u + 2, :])
+        def load_wg(lo, hi):
+            rows = keep.tile([P, hi - lo, S], F32, name="wg%d" % lo)
+            for q in (0, 2, 1, 3):
+                nc.sync.dma_start(out=rows[32 * q : 32 * q + 32, :, :], in_=wgs.rearrange("(p t) j -> p t j", t=PACK)[:, lo:hi, :])
+            for t in range(lo, hi):
+                wg[t] = rows[:, t - lo, :]
 
         w1_raw = {}
 
@@ -102,10 +103,11 @@ def tile_list_dive_profile_scores_kernel(
         load_w1(1, 0)
         nc.sync.dma_start(out=w4_raw[:].bitcast(I32), in_=w4_words.rearrange("a p n -> p a n").bitcast(I32))
         load_w1(2, 0)
-        load_wg(0)
+        load_wg(0, 1)
         load_page(0)
+        load_wg(1, 2)
         load_page(1)
-        load_wg(1)
+        load_wg(2, 4)
         load_w1(0, 1)
         load_w1(1, 1)
         load_page(2)
@@ -217,7 +219,7 @@ def tile_list_dive_profile_scores_kernel(
         CH = 256
 
         def put(s):
-            nc.vector.tensor_tensor(page[s][:].indirect(idx2[:]), h[s][:], wg[s % PACK // 2][:, s % 2, :], ALU.mult)
+            nc.vector.tensor_tensor(page[s][:].indirect(idx2[:]), h[s][:], wg[s % PACK], ALU.mult)
 
         def fetch(s, xg):
             nc.vector.tensor_copy(xg[:, s % PACK, :], page[s][:].indirect(idx3[:]))
@@ -316,7 +318,7 @@ def tile_list_dive_profile_scores_kernel(
             quantise_page(1, pbf1, c)
 
         for mt in range(MT):
-            acc = psum.tile([P, NP], F32, name="acc", tag="pb" if mt < MT // 2 else "pa")
+            acc = psum.tile([P, NP], F32, name="acc", tag=("po", "pp", "pb", "pa")[mt // 2])
             for b in range(HB):
                 nc.tensor.matmul_mx(
                     out=acc[:], lhsT=p_w[:, b, mt * P : (mt + 1) * P].bitcast(FP8X4), lhsT_scale=p_sc[b][:, mt * P : (mt + 1) * P],

from contextlib import ExitStack

import concourse.mybir as mybir

K, T, S, H, T2, NP = 1536, 2048, 512, 1024, 1024, 512
FLOPS = 2 * K * H * S * 2 + 2 * H * T2 * NP

F32 = mybir.dt.float32
BF16 = mybir.dt.bfloat16
I32 = mybir.dt.int32
U32 = mybir.dt.uint32
U16 = mybir.dt.uint16
U8 = mybir.dt.uint8
FP8X4 = mybir.dt.float8_e4m3fn_x4
FP4X4 = mybir.dt.float4_e2m1fn_x4
ALU = mybir.AluOpType
ACT = mybir.ActivationFunctionType

P = 128
PACK = 4
KP = P * PACK
KA = K // KP
HB = H // KP
MT = T2 // P


def tile_list_dive_profile_scores_kernel(
    tc, tab_words, tab_scales, offs, w1, w4_words, w4_scales, page0, wgs, offs2, offs3, cen, wv, slot, out
):
    nc = tc.nc
    with ExitStack() as ctx:
        keep = ctx.enter_context(tc.tile_pool(name="keep", bufs=1))
        ring = ctx.enter_context(tc.tile_pool(name="ring", bufs=1))
        psum = ctx.enter_context(tc.psum_pool(name="psum", bufs=2))

        idx1 = keep.tile([P, S // 16], U16, name="idx1")
        idx2 = keep.tile([P, S // 16], U16, name="idx2")
        idx3 = keep.tile([P, NP // 16], U16, name="idx3")

        tab_sc = keep.tile([P, KA, T], U8, name="tab_sc", align_bytes=64)
        w4_sc_raw = keep.tile([P, KA, H], U8, name="w4_sc_raw", align_bytes=64)
        tab_sc_words = tab_sc[:].rearrange("p a n -> p (a n)").bitcast(I32)
        nc.gpsimd.memset(tab_sc_words[:, 0:768], 0)
        nc.vector.memset(tab_sc_words[:, 768:], 0)
        nc.vector.memset(w4_sc_raw[:].bitcast(I32), 0)
        warm = keep.tile([P, 1], F32, name="warm")
        nc.gpsimd.memset(warm[:], 1.0)
        warm2 = keep.tile([P, 1], F32, name="warm2")
        nc.scalar.activation(out=warm2[:], in_=warm[:], func=ACT.Ln, bias=1.0)


        nc.sync.dma_start(idx1[:], offs)
        nc.sync.dma_start(idx2[:], offs2)
        nc.sync.dma_start(idx3[:], offs3)
        cen_sb = keep.tile([P, HB, PACK], F32, name="cen_sb")
        wv_sb = keep.tile([P, HB, PACK], F32, name="wv_sb")
        slot_sb = keep.tile([P, MT], F32, name="slot_sb")
        tab_w = [ring.tile([P, T], U32, name="tab_w%d" % a, tag="t%d" % a, align_bytes=64) for a in range(KA)]
        w4_raw = keep.tile([P, KA, 2 * H], U8, name="w4_raw", align_bytes=64)

        def load_tab(a, lo, hi):
            nc.sync.dma_start(out=tab_w[a][:, lo:hi].bitcast(I32), in_=tab_words[a].rearrange("p n i -> p (n i)").bitcast(I32)[:, lo:hi])

        for c in range(4):
            load_tab(0, c * T // 4, (c + 1) * T // 4)
        for r in range(4):
            nc.sync.dma_start(
                out=tab_sc[r:P:32, :, :].bitcast(I32), in_=tab_scales.rearrange("a (q r) n -> r q a n", r=4)[r].bitcast(I32)
            )
        load_tab(1, 0, T)
        for r in range(4):
            nc.sync.dma_start(
                out=w4_sc_raw[r:P:32, :, :].bitcast(I32), in_=w4_scales.rearrange("a (q r) n -> r q a n", r=4)[r].bitcast(I32)
            )
        load_tab(2, 0, T)
        wg = {}

        def load_wg(lo, hi):
            rows = keep.tile([P, hi - lo, S], F32, name="wg%d" % lo)
            for q in (0, 2, 1, 3):
                nc.sync.dma_start(out=rows[32 * q : 32 * q + 32, :, :], in_=wgs.rearrange("(p t) j -> p t j", t=PACK)[:, lo:hi, :])
            for t in range(lo, hi):
                wg[t] = rows[:, t - lo, :]

        w1_raw = {}

        def load_w1(a, b):
            raw = ring.tile([P, PACK, KP], F32, name="w1_raw%d%d" % (a, b), tag=("w%d" if b == 0 else "t%d") % a, align_bytes=64)
            nc.sync.dma_start(
                out=raw[:], in_=w1[a * KP : (a + 1) * KP, b * KP : (b + 1) * KP].rearrange("(p j) c -> p j c", j=PACK)
            )
            w1_raw[(a, b)] = raw

        page = {}

        def load_page(s):
            b, t = divmod(s, PACK)
            pg = keep.tile([P, T2], F32, name="page%d" % s)
            nc.sync.dma_start(out=pg[:], in_=page0[b * KP : (b + 1) * KP, :].rearrange("(p t) m -> p t m", t=PACK)[:, t, :])
            page[s] = pg

        load_w1(0, 0)
        load_w1(1, 0)
        nc.sync.dma_start(out=w4_raw[:].bitcast(I32), in_=w4_words.rearrange("a p n -> p a n").bitcast(I32))
        load_w1(2, 0)
        load_wg(0, 1)
        load_page(0)
        load_wg(1, 2)
        load_page(1)
        load_wg(2, 4)
        load_w1(0, 1)
        load_w1(1, 1)
        load_page(2)
        load_w1(2, 1)
        nc.sync.dma_start(out=cen_sb[:], in_=cen.rearrange("(b p t) -> p b t", b=HB, t=PACK))
        nc.sync.dma_start(out=wv_sb[:], in_=wv.rearrange("(b p t) -> p b t", b=HB, t=PACK))
        for s in range(3, HB * PACK):
            load_page(s)
        with nc.allow_non_contiguous_dma(reason="one bound for each partition"):
            nc.sync.dma_start(out=slot_sb[:], in_=slot.rearrange("(c p) -> p c", p=P))

        v_w = keep.tile([P, KA, S], U32, name="v_w", align_bytes=64)
        v_sc = keep.tile([P, KA, S], U8, name="v_sc", align_bytes=64)
        w4_w = keep.tile([P, KA, 2 * H], U8, name="w4_w", align_bytes=64)
        w4_sc = keep.tile([P, KA, H], U8, name="w4_sc", align_bytes=64)

        def deal_words(b):
            nc.vector.tensor_copy(
                out=w4_w[:].bitcast(U16).rearrange("p a (b t m) -> p b a t m", b=HB, t=PACK)[:, b],
                in_=w4_raw[:].bitcast(U16).rearrange("p a (b m t) -> p b a t m", b=HB, t=PACK)[:, b],
            )

        def deal_scales(b):
            nc.vector.tensor_copy(
                out=w4_sc[:].rearrange("p a (b t m) -> p b a t m", b=HB, t=PACK)[:, b],
                in_=w4_sc_raw[:].rearrange("p a (b m t) -> p b a t m", b=HB, t=PACK)[:, b],
            )

        def gather_words(a):
            nc.vector.tensor_copy(v_w[:, a, :], tab_w[a][:].indirect(idx1[:]))

        def gather_scales(a):
            nc.vector.tensor_copy(v_sc[:, a, :], tab_sc[:, a, :].indirect(idx1[:]))

        gather_words(0)
        gather_scales(0)
        gather_scales(1)
        gather_words(1)
        gather_scales(2)
        deal_scales(0)
        gather_words(2)
        deal_scales(1)

        w1_w = keep.tile([P, KA, HB, KP], U32, name="w1_w", align_bytes=64)
        w1_sc = keep.tile([P, KA, HB, KP], U8, name="w1_sc", align_bytes=64)

        def quantise_w1(a, b, wbf):
            nc.vector.quantize_mx(out=w1_w[:, a, b, :].bitcast(FP8X4), scales=w1_sc[:, a, b, :], in_=wbf[:])

        def prep_w1(a, b):
            wbf = ring.tile([P, KP * PACK], BF16, name="wbf", tag="bf", bufs=3, align_bytes=64)
            dst = wbf[:].rearrange("p (t m j) -> p m j t", t=PACK, j=PACK)
            src = w1_raw[(a, b)][:].rearrange("p j (m t) -> p m j t", t=PACK)
            if b == 0 and a == KA - 1:
                nc.vector.tensor_copy(out=dst[:, :, :, 0], in_=src[:, :, :, 0])
                nc.vector.quantize_mx(out=w1_w[:, a, b, 0:P].bitcast(FP8X4), scales=w1_sc[:, a, b, 0:P], in_=wbf[:, 0:KP])

                def rest():
                    nc.vector.tensor_copy(out=dst[:, :, :, 1:PACK], in_=src[:, :, :, 1:PACK])
                    nc.vector.quantize_mx(out=w1_w[:, a, b, P : 2 * P].bitcast(FP8X4), scales=w1_sc[:, a, b, P : 2 * P], in_=wbf[:, KP : 2 * KP])
                    nc.vector.quantize_mx(out=w1_w[:, a, b, 2 * P :].bitcast(FP8X4), scales=w1_sc[:, a, b, 2 * P :], in_=wbf[:, 2 * KP :])

                return rest
            nc.scalar.copy(out=dst, in_=src)
            quantise_w1(a, b, wbf)

        h = {}

        def first_product(s, after=None):
            b, t = divmod(s, PACK)
            acc = psum.tile([P, S], F32, name="acc", tag="pa")
            for a in range(KA):
                nc.tensor.matmul_mx(
                    out=acc[:], lhsT=w1_w[:, a, b, t * P : (t + 1) * P].bitcast(FP8X4), lhsT_scale=w1_sc[:, a, b, t * P : (t + 1) * P],
                    rhs=v_w[:, a, :].bitcast(FP8X4), rhs_scale=v_sc[:, a, :], start=(a == 0), stop=(a == KA - 1),
                )
            h[s] = lw[s] if after is None else ring.tile([P, S], F32, name="h", tag=after, align_bytes=64)
            nc.vector.tensor_tensor(out=h[s][:], in0=acc[:], in1=lw[s][:], op=ALU.mult)

        lw = {}

        def second_product(s):
            b, t = divmod(s, PACK)
            acc = psum.tile([P, S], F32, name="acc", tag="pb")
            for a in range(KA):
                nc.tensor.matmul_mx(
                    out=acc[:], lhsT=w4_w[:, a, s * 2 * P : (s + 1) * 2 * P].bitcast(FP4X4), lhsT_scale=w4_sc[:, a, s * P : (s + 1) * P],
                    rhs=v_w[:, a, :].bitcast(FP8X4), rhs_scale=v_sc[:, a, :], start=(a == 0), stop=(a == KA - 1),
                )
            sq = ring.tile([P, S], F32, name="sq", tag="sq", bufs=2)
            nc.scalar.activation(out=sq[:], in_=acc[:], func=ACT.Square)
            f = ring.tile([P, S], F32, name="lw", tag="h%d" % s, align_bytes=64)
            nc.scalar.activation(out=f[:], in_=sq[:], func=ACT.Ln, bias=1.0)
            lw[s] = f

        prep_w1(0, 0)
        prep_w1(1, 0)
        deal_words(0)
        second_product(0)
        rest_of_w1 = prep_w1(2, 0)
        first_product(0)
        second_product(1)


        p_w = keep.tile([P, HB, T2], U32, name="p_w", align_bytes=64)
        x_w = keep.tile([P, HB, NP], U32, name="x_w", align_bytes=64)
        p_sc = [keep.tile([P, T2], U8, name="p_sc%d" % b, align_bytes=64) for b in range(HB)]
        x_sc = [keep.tile([P, NP], U8, name="x_sc%d" % b, align_bytes=64) for b in range(HB)]
        CH = 256

        def put(s):
            nc.vector.tensor_tensor(page[s][:].indirect(idx2[:]), h[s][:], wg[s % PACK], ALU.mult)

        def fetch(s, xg):
            nc.vector.tensor_copy(xg[:, s % PACK, :], page[s][:].indirect(idx3[:]))

        def centre(s, xc, xg):
            b, t = divmod(s, PACK)
            nc.scalar.activation(out=xc[:, t, :], in_=xg[:, t, :], func=ACT.Identity, bias=nb[:, b, t : t + 1], scale=wv_sb[:, b, t : t + 1])

        def weave(copy, dst, src):
            copy(out=dst.rearrange("p (c i t) -> p c t i", i=4, t=PACK), in_=src.rearrange("p t (c i) -> p c t i", i=4))

        def quantise_page(b, pbf, c):
            nc.vector.quantize_mx(
                out=p_w[:, b, c * CH : (c + 1) * CH].bitcast(FP8X4), scales=p_sc[b][:, c * CH : (c + 1) * CH],
                in_=pbf[:, c * CH * PACK : (c + 1) * CH * PACK],
            )

        stage0 = ring.tile([P, PACK, T2], F32, name="stage0", tag="stage0", align_bytes=64)
        stage1 = [ring.tile([P, 2, T2], F32, name="stage1%d" % u) for u in range(2)]
        xg0 = ring.tile([P, PACK, NP], F32, name="xg", tag="w0", align_bytes=64)
        xg1 = ring.tile([P, PACK, NP], F32, name="xg", tag="w1", align_bytes=64)

        def step(s, xg, staged):
            put(s)
            nc.sync.dma_start(out=staged, in_=page[s][:])
            fetch(s, xg)

        def weave_pair(u, lo, hi):
            nc.scalar.copy(
                out=pbf1[:, lo * PACK : hi * PACK].rearrange("p (c i u e) -> p u c e i", i=4, u=2, e=2)[:, u],
                in_=stage1[u][:, :, lo:hi].rearrange("p e (c i) -> p c e i", i=4),
            )

        step(0, xg0, stage0[:, 0, :])
        rest_of_w1()
        deal_words(1)
        first_product(1)
        step(1, xg0, stage0[:, 1, :])
        second_product(2)
        first_product(2)
        step(2, xg0, stage0[:, 2, :])
        for a in range(KA):
            prep_w1(a, 1)
        second_product(3)
        first_product(3)
        step(3, xg0, stage0[:, 3, :])
        nb = ring.tile([P, HB, PACK], F32, name="nb", tag="h2", align_bytes=64)
        nc.vector.scalar_tensor_tensor(out=nb[:], in0=cen_sb[:], scalar=-1.0, in1=wv_sb[:], op0=ALU.mult, op1=ALU.mult)
        second_product(4)
        first_product(4)
        second_product(5)
        xc0 = ring.tile([P, PACK, NP], BF16, name="xc0", tag="t2", align_bytes=64)
        for s in range(PACK - 1):
            centre(s, xc0, xg0)
        step(4, xg1, stage1[0][:, 0, :])
        first_product(5)
        second_product(6)
        centre(3, xc0, xg0)
        xbf0 = ring.tile([P, NP * PACK], BF16, name="xbf0", tag="xbf0", align_bytes=64)
        weave(nc.scalar.copy, xbf0[:], xc0[:])
        second_product(7)
        pbf0 = ring.tile([P, T2 * PACK], BF16, name="pbf0", tag="pbf0", align_bytes=64)
        for c in range(T2 // CH):
            weave(nc.scalar.copy, pbf0[:, c * CH * PACK : (c + 1) * CH * PACK], stage0[:, :, c * CH : (c + 1) * CH])
        step(5, xg1, stage1[0][:, 1, :])
        nc.vector.quantize_mx(out=x_w[:, 0, :].bitcast(FP8X4), scales=x_sc[0][:], in_=xbf0[:])
        first_product(6, after="xbf0")
        x_late = ring.tile([P, (2 + PACK) * NP], BF16, name="x_late", tag="stage0", align_bytes=64)
        xc1 = x_late[:, 0 : 2 * NP].rearrange("p (e c) -> p e c", e=2)
        xbf1 = x_late[:, 2 * NP :]
        centre(4, xc1, xg1)
        centre(5, xc1, xg1)
        pbf1 = ring.tile([P, T2 * PACK], BF16, name="pbf1", align_bytes=64)
        weave_pair(0, 0, T2)
        step(6, xg1, stage1[1][:, 0, :])
        nc.vector.quantize_mx(out=p_w[:, 0, :].bitcast(FP8X4), scales=p_sc[0][:], in_=pbf0[:])
        first_product(7, after="pbf0")
        nc.scalar.copy(
            out=xbf1.rearrange("p (c i u e) -> p u c e i", i=4, u=2, e=2)[:, 0],
            in_=xc1.rearrange("p e (c i) -> p c e i", i=4),
        )
        nc.scalar.activation(
            out=xbf1.rearrange("p (c t) -> p c t", t=PACK)[:, :, 2:4], in_=xg1[:, 2, :].unsqueeze(2).to_broadcast([P, NP, 2]),
            func=ACT.Identity, bias=nb[:, 1, 2:3], scale=wv_sb[:, 1, 2:3],
        )
        put(7)
        fetch(7, xg1)
        nc.vector.tensor_scalar(
            out=xbf1.rearrange("p (c t) -> p c t", t=PACK)[:, :, 3], in0=xg1[:, 3, :],
            scalar1=cen_sb[:, 1, 3:4], scalar2=wv_sb[:, 1, 3:4], op0=ALU.subtract, op1=ALU.mult,
        )
        nc.vector.quantize_mx(out=x_w[:, 1, :].bitcast(FP8X4), scales=x_sc[1][:], in_=xbf1)
        for c in range(T2 // CH):
            nc.scalar.copy(out=stage1[1][:, 1, c * CH : (c + 1) * CH], in_=page[7][:, c * CH : (c + 1) * CH])
            weave_pair(1, c * CH, (c + 1) * CH)
            quantise_page(1, pbf1, c)

        for mt in range(MT):
            acc = psum.tile([P, NP], F32, name="acc", tag=("po", "pp", "pb", "pa")[mt // 2])
            for b in range(HB):
                nc.tensor.matmul_mx(
                    out=acc[:], lhsT=p_w[:, b, mt * P : (mt + 1) * P].bitcast(FP8X4), lhsT_scale=p_sc[b][:, mt * P : (mt + 1) * P],
                    rhs=x_w[:, b, :].bitcast(FP8X4), rhs_scale=x_sc[b][:], start=(b == 0), stop=(b == HB - 1),
                )
            res = ring.tile([P, NP], F32, name="res", tag="h%d" % mt, align_bytes=64)
            if mt >= 3:
                nc.scalar.copy(out=res[:], in_=acc[:])
                nc.vector.tensor_scalar(out=res[:], in0=res[:], scalar1=slot_sb[:, mt : mt + 1], scalar2=None, op0=ALU.max)
            else:
                nc.vector.tensor_scalar(out=res[:], in0=acc[:], scalar1=slot_sb[:, mt : mt + 1], scalar2=None, op0=ALU.max)
            nc.sync.dma_start(out=out[mt * P : (mt + 1) * P, :], in_=res[:])
